import numpy as np
import ml_dtypes


def mxq(x, axis, fmt="e4m3"):
    dtype, down = {"e4m3": (ml_dtypes.float8_e4m3fn, 7), "e5m2": (ml_dtypes.float8_e5m2, 14)}[fmt]
    v = np.moveaxis(np.asarray(x, np.float32).astype(ml_dtypes.bfloat16).astype(np.float64), axis, -1)
    blocks = v.reshape(v.shape[:-1] + (-1, 32))
    amax = np.abs(blocks).max(-1, keepdims=True)
    byte = np.maximum(np.where(amax > 0, np.frexp(amax)[1] - 1 + 127, 0) - down, 1)
    scale = np.exp2(byte - 127.0)
    codes = (blocks / scale).astype(np.float32).astype(dtype).astype(np.float64)
    return np.moveaxis((codes * scale).reshape(v.shape), -1, axis)


WIDE = False


def mx_kscale(k, group=512):
    if not WIDE:
        return np.ones(k)
    levels = np.array([10, -10, 5, -5, 0])
    if group != 512:
        return np.exp2(np.random.permutation(np.resize(levels, k // group))).repeat(group)
    if k % 512:
        return np.exp2(np.random.permutation(np.resize(levels, k // 32))).repeat(32)
    a = np.empty((k // 512, 16))
    for p in range(k // 512):
        a[p, :8] = np.random.permutation(np.resize(levels, 8))
        for g in range(8):
            far = levels[np.abs(levels - a[p, g]) >= 10]
            a[p, g + 8] = far[np.random.randint(len(far))]
    return np.exp2(a.ravel()).repeat(32)


def f64(x):
    return np.asarray(x).astype(np.float64)


def striped(idx):
    return np.tile(np.asarray(idx).reshape(-1, 16).T, (8, 1)).astype(np.uint16)


def unstriped(offs):
    return offs[:16].T.reshape(-1).astype(np.int64)


H, KV, D, NQ, N = 8, 2, 128, 512, 512


def setup_inputs():
    n = np.random.standard_normal
    s = mx_kscale(D, 0)[:, None]
    u = mx_kscale(N)
    t = np.random.uniform(0.5, 2.0, N) * u
    v = n((KV, N, 128))
    return {
        "qT": (n((H, D, NQ)) * s * (0.70 / np.sqrt(D))).astype(np.float32),
        "kT": (n((KV, D, N)) / s).astype(np.float32),
        "t": t.reshape(N, 1).astype(np.float32),
        "v": (v / t[:, None]).astype(np.float32),
        "mask": (np.arange(N)[:, None] <= np.sort(np.random.randint(N // 4, N, NQ))[None, :]).astype(np.float32),
    }


def reference(qT, kT, t, v, mask):
    a = np.repeat(mxq(f64(kT), 1, "e4m3"), H // KV, 0).transpose(0, 2, 1) @ mxq(f64(qT), 1, "e4m3")
    p = np.maximum(a, 0.0)
    p = p * f64(mask)
    w = p * f64(t)
    y = mxq(w, 1, "e4m3").transpose(0, 2, 1) @ np.repeat(mxq(f64(v), 1, "e4m3"), H // KV, 0)
    y = y / 16.0
    return y

@@ -1,0 +1,259 @@
+from contextlib import ExitStack
+
+import concourse.mybir as mybir
+
+H, KV, D, NQ, N = 8, 2, 128, 512, 512
+FLOPS = 2 * 2 * H * NQ * N * D
+
+F32 = mybir.dt.float32
+BF16 = mybir.dt.bfloat16
+U32 = mybir.dt.uint32
+U8 = mybir.dt.uint8
+FP8X4 = mybir.dt.float8_e4m3fn_x4
+ACT = mybir.ActivationFunctionType
+ALU = mybir.AluOpType
+
+P = 128
+PACK = 4
+ROWS = 32
+TILES = 4
+QT = 128
+GROUPS = 8
+SETS = ((2, 3, 4, 5), (0, 1, 6, 7))
+OUT_SCALE = 1.0 / 16.0
+
+
+def tile_rows_a_relu_mask_kernel(tc, qT, kT, t, v, mask, out):
+    nc = tc.nc
+    with ExitStack() as ctx:
+        sb = ctx.enter_context(tc.tile_pool(name="sb", bufs=1))
+        ps = ctx.enter_context(tc.psum_pool(name="ps", bufs=1))
+        ctx.enter_context(tc.manual_schedule())
+
+        def tile(name, shape, dtype):
+            return sb.tile(shape, dtype, name=name, align_bytes=64)
+
+        chunks = ((0, 128), (128, 128), (256, 256))
+        k_raw = tile("k_raw", [P, PACK, N], F32)
+        t_sb = tile("t_sb", [P, PACK], F32)
+        v_raw = tile("v_raw", [P, KV, PACK, D], F32)
+        q_raw = [[tile("q_raw%d%d" % (s, n), [P, PACK, w], F32) for n, (c0, w) in enumerate(chunks)] for s in range(2)]
+        m_raw = [tile("m_raw%d" % n, [P, PACK, w], F32) for n, (c0, w) in enumerate(chunks)]
+        m_scaled = [tile("m_scaled%d" % n, [P, PACK, w], F32) for n, (c0, w) in enumerate(chunks)]
+        mt = [tile("mt%d" % c, [P, QT, PACK], F32) for c in range(4)]
+        k_bf = tile("k_bf", [P, PACK, P, PACK], BF16)
+        k_codes = tile("k_codes", [P, N], U32)
+        k_scales = tile("k_scales", [P, N], U8)
+        q_bf = tile("q_bf", [P, GROUPS, QT, PACK], BF16)
+        q_codes = tile("q_codes", [P, GROUPS * QT], U32)
+        q_scales = tile("q_scales", [P, GROUPS * QT], U8)
+        v_bf = tile("v_bf", [P, KV, D, PACK], BF16)
+        v_codes = tile("v_codes", [P, KV * D], U32)
+        v_scales = tile("v_scales", [P, KV * D], U8)
+        w_bf = tile("w_bf", [P, TILES, QT, PACK], BF16)
+        w_codes = tile("w_codes", [P, GROUPS, TILES * QT], U32)
+        w_scales = tile("w_scales", [P, GROUPS, TILES * QT], U8)
+        p_f32 = [tile("p_f32_%d" % n, [P, QT, PACK], F32) for n in range(2)]
+        y_sb = [tile("y_sb%d" % i, [P, TILES, D], F32) for i in range(GROUPS)]
+
+        nbanks = (1, 2, 2, 1)
+        s_banks = [[ps.tile([P, PACK, QT], F32, name="s%d%d" % (g, n)) for n in range(nbanks[g])] for g in range(TILES)]
+        y_banks = [ps.tile([P, TILES, D], F32, name="y%d" % n) for n in range(2)]
+
+        def s_bank(i, g):
+            return s_banks[g][i % nbanks[g]]
+
+        def window(tiles, c):
+            n = min(c, 2)
+            lo = c * QT - chunks[n][0]
+            return tiles[n][:, :, lo : lo + QT]
+
+        def load_q(s, n):
+            c0, w = chunks[n]
+            heads = SETS[s]
+            runs = ((0, 4),) if s == 0 else ((0, 2), (2, 2))
+            for g0, count in runs:
+                src = qT[heads[g0] : heads[g0] + count, :, c0 : c0 + w].rearrange("h (p j) q -> (h p) j q", j=PACK)
+                nc.sync.dma_start(out=q_raw[s][n][g0 * ROWS : (g0 + count) * ROWS], in_=src)
+
+        def load_mask(n):
+            c0, w = chunks[n]
+            nc.sync.dma_start(out=m_raw[n][:], in_=mask[:, c0 : c0 + w].rearrange("(p r) q -> p r q", r=PACK))
+
+        for g, queue in ((0, nc.sync), (2, nc.scalar), (1, nc.sync), (3, nc.scalar)):
+            queue.dma_start(out=k_raw[g * ROWS : (g + 1) * ROWS], in_=kT[g // 2].rearrange("(p j) n -> p j n", j=PACK))
+        nc.scalar.dma_start(out=t_sb[:], in_=t.rearrange("(p r) o -> p (r o)", r=PACK))
+        load_q(0, 0)
+        load_mask(0)
+        load_q(1, 0)
+        load_q(0, 1)
+        load_mask(1)
+        load_q(1, 1)
+        nc.sync.dma_start(out=v_raw[:], in_=v.rearrange("k (p r) e -> p k r e", r=PACK))
+        load_q(0, 2)
+        load_mask(2)
+        load_q(1, 2)
+
+        def quantize(codes, scales, src):
+            nc.vector.quantize_mx(out=codes.bitcast(FP8X4), scales=scales, in_=src)
+
+        def interleave(dst, src):
+            nc.scalar.activation(
+                out=dst.rearrange("p (c i) j -> p c j i", i=4),
+                in_=src.rearrange("p j (c i) -> p c j i", i=4),
+                func=ACT.Copy,
+            )
+
+        def interleave_q(i):
+            interleave(q_bf[:, i], window(q_raw[i % 2], i // 2))
+
+        def quantize_q(i, count=1):
+            cols = slice(i * QT, (i + count) * QT)
+            quantize(q_codes[:, cols], q_scales[:, cols], q_bf[:, i : i + count].rearrange("p g q j -> p (g q j)"))
+
+        def scale_mask(n):
+            for r in range(PACK):
+                nc.scalar.activation(out=m_scaled[n][:, r], in_=m_raw[n][:, r], func=ACT.Copy, scale=t_sb[:, r : r + 1])
+
+        def interleave_mask(c):
+            nc.scalar.activation(
+                out=mt[c][:].rearrange("p (c i) r -> p c r i", i=2),
+                in_=window(m_scaled, c).rearrange("p r (c i) -> p c r i", i=2),
+                func=ACT.Copy,
+            )
+
+        def scores(i):
+            cols = slice(i * QT, (i + 1) * QT)
+            for r in range(PACK):
+                keys = slice(r * P, (r + 1) * P)
+                for g in (0, 3, 1, 2):
+                    rows = slice(g * ROWS, (g + 1) * ROWS)
+                    nc.tensor.matmul_mx(
+                        out=s_bank(i, g)[:, r],
+                        lhsT=k_codes[rows, keys].bitcast(FP8X4),
+                        lhsT_scale=k_scales[rows, keys],
+                        rhs=q_codes[rows, cols].bitcast(FP8X4),
+                        rhs_scale=q_scales[rows, cols],
+                        start=True,
+                        stop=True,
+                    )
+
+        def weights_vector(i, g):
+            nc.vector.scalar_tensor_tensor(
+                out=w_bf[:, g],
+                in0=s_bank(i, g)[:].rearrange("p r q -> p q r"),
+                scalar=0.0,
+                in1=mt[i // 2][:],
+                op0=ALU.max,
+                op1=ALU.mult,
+            )
+
+        def relu_scalar(i):
+            nc.scalar.activation(out=p_f32[i % 2][:], in_=s_bank(i, 3)[:].rearrange("p r q -> p q r"), func=ACT.Relu)
+
+        def weights_gpsimd(i):
+            nc.gpsimd.tensor_tensor(out=w_bf[:, 3], in0=p_f32[i % 2][:], in1=mt[i // 2][:], op=ALU.mult)
+
+        def quantize_w(i):
+            for g0 in (0, 2):
+                cols = slice(g0 * QT, (g0 + 2) * QT)
+                quantize(w_codes[:, i, cols], w_scales[:, i, cols], w_bf[:, g0 : g0 + 2].rearrange("p g q r -> p (g q r)"))
+
+        def y_bank(i, g):
+            return y_banks[(i + (g // 2 if i == GROUPS - 1 else 0)) % 2]
+
+        def values(i, tiles=range(TILES)):
+            for g in tiles:
+                cols = slice(g * QT, (g + 1) * QT)
+                feats = slice(g // 2 * D, (g // 2 + 1) * D)
+                nc.tensor.matmul_mx(
+                    out=y_bank(i, g)[:, g],
+                    lhsT=w_codes[:, i, cols].bitcast(FP8X4),
+                    lhsT_scale=w_scales[:, i, cols],
+                    rhs=v_codes[:, feats].bitcast(FP8X4),
+                    rhs_scale=v_scales[:, feats],
+                    start=True,
+                    stop=True,
+                )
+
+        def store(i, g0, count):
+            h0 = SETS[i % 2][g0]
+            rows = slice(i // 2 * QT, (i // 2 + 1) * QT)
+            nc.sync.dma_start(out=out[h0 : h0 + count, rows, :].rearrange("h q e -> q h e"), in_=y_sb[i][:, g0 : g0 + count])
+
+        def finish(i):
+            nc.scalar.activation(out=y_sb[i][:], in_=y_bank(i, 0)[:], func=ACT.Copy, scale=OUT_SCALE)
+            if i % 2 == 0:
+                store(i, 0, 4)
+            else:
+                store(i, 0, 2)
+                store(i, 2, 2)
+
+        k_in = k_raw[:].rearrange("p j (s r) -> p s j r", r=PACK)
+        k_out = k_bf[:].rearrange("p r s j -> p s j r")
+        nc.vector.tensor_copy(out=k_out[:, :, :, 0:3], in_=k_in[:, :, :, 0:3])
+        nc.scalar.activation(out=k_bf[:, 3], in_=k_in[:, :, :, 3], func=ACT.Copy)
+        interleave_q(0)
+        quantize(k_codes[:], k_scales[:], k_bf[:].rearrange("p r s j -> p (r s j)"))
+        quantize_q(0)
+        scores(0)
+        nc.vector.tensor_tensor(
+            out=mt[0][:].rearrange("p (c i) r -> p c r i", i=2),
+            in0=m_raw[0][:].rearrange("p r (c i) -> p c r i", i=2),
+            in1=t_sb[:].unsqueeze(1).unsqueeze(3).to_broadcast([P, QT // 2, PACK, 2]),
+            op=ALU.mult,
+        )
+        relu_scalar(0)
+        weights_gpsimd(0)
+        interleave_q(1)
+        interleave_q(2)
+        for g in range(3):
+            weights_vector(0, g)
+        quantize_q(1, 2)
+        scores(1)
+        quantize_w(0)
+        scale_mask(1)
+        interleave_mask(1)
+        relu_scalar(1)
+
+        def v_half(k):
+            interleave(v_bf[:, k], v_raw[:, k])
+
+        def step(i, pe_before, scalar_before, pe_after, scalar_after):
+            weights_gpsimd(i)
+            weights_vector(i, 0)
+            for work in pe_before:
+                work()
+            if i + 1 < GROUPS:
+                scores(i + 1)
+            if i + 2 < GROUPS:
+                interleave_q(i + 2)
+            for work in scalar_before:
+                work()
+            if i + 1 < GROUPS:
+                relu_scalar(i + 1)
+            for work in pe_after:
+                work()
+            for work in scalar_after:
+                work()
+            weights_vector(i, 1)
+            weights_vector(i, 2)
+            if i + 2 < GROUPS:
+                quantize_q(i + 2)
+            if i == 2:
+                quantize(v_codes[:], v_scales[:], v_bf[:].rearrange("p k e r -> p (k e r)"))
+            quantize_w(i)
+
+        step(1, [], [], [], [lambda: v_half(0), lambda: v_half(1)])
+        step(2, [], [], [], [lambda: scale_mask(2)])
+        step(3, [lambda: values(0), lambda: values(1)], [lambda: finish(0)], [lambda: values(2)], [lambda: interleave_mask(2)])
+        step(4, [], [lambda: finish(1)], [lambda: values(3)], [lambda: finish(2)])
+        step(5, [lambda: values(4)], [lambda: finish(3)], [], [lambda: interleave_mask(3)])
+        step(6, [lambda: values(5)], [lambda: finish(4)], [], [lambda: finish(5)])
+        step(7, [lambda: values(6)], [lambda: finish(6)], [], [])
+        last = GROUPS - 1
+        values(last)
+        nc.scalar.activation(out=y_sb[last][:, 0:2], in_=y_bank(last, 0)[:, 0:2], func=ACT.Copy, scale=OUT_SCALE)
+        store(last, 0, 2)
+        nc.vector.tensor_scalar_mul(y_sb[last][:, 2:4], y_bank(last, 2)[:, 2:4], OUT_SCALE)
+        store(last, 2, 2)

@@ -21,6 +21,7 @@ QT = 128
 GROUPS = 8
 SETS = ((2, 3, 4, 5), (0, 1, 6, 7))
 OUT_SCALE = 1.0 / 16.0
+WARM_HEAD = 48
 
 
 def tile_rows_a_relu_mask_kernel(tc, qT, kT, t, v, mask, out):
@@ -56,9 +57,27 @@ def tile_rows_a_relu_mask_kernel(tc, qT, kT, t, v, mask, out):
         p_f32 = [tile("p_f32_%d" % n, [P, QT, PACK], F32) for n in range(2)]
         y_sb = [tile("y_sb%d" % i, [P, TILES, D], F32) for i in range(GROUPS)]
 
-        nbanks = (1, 2, 2, 1)
+        nbanks = (2, 1, 1, 1)
         s_banks = [[ps.tile([P, PACK, QT], F32, name="s%d%d" % (g, n)) for n in range(nbanks[g])] for g in range(TILES)]
         y_banks = [ps.tile([P, TILES, D], F32, name="y%d" % n) for n in range(2)]
+
+        spare_bank = ps.tile([P, TILES, D], F32, name="spare")
+        z_bf = tile("z_bf", [P, 512], BF16)
+        z_codes = tile("z_codes", [P, P], U32)
+        z_scales = tile("z_scales", [P, P], U8)
+        z_act = tile("z_act", [P, 1], F32)
+
+        def keep_warm(count):
+            for n in range(count):
+                nc.tensor.matmul_mx(
+                    out=spare_bank[:, n % TILES],
+                    lhsT=z_codes[:].bitcast(FP8X4),
+                    lhsT_scale=z_scales[:],
+                    rhs=z_codes[:].bitcast(FP8X4),
+                    rhs_scale=z_scales[:],
+                    start=True,
+                    stop=True,
+                )
 
         def s_bank(i, g):
             return s_banks[g][i % nbanks[g]]
@@ -122,11 +141,11 @@ def tile_rows_a_relu_mask_kernel(tc, qT, kT, t, v, mask, out):
                 func=ACT.Copy,
             )
 
-        def scores(i):
+        def scores(i, tiles):
             cols = slice(i * QT, (i + 1) * QT)
-            for r in range(PACK):
-                keys = slice(r * P, (r + 1) * P)
-                for g in (0, 3, 1, 2):
+            for g in tiles:
+                for r in range(PACK):
+                    keys = slice(r * P, (r + 1) * P)
                     rows = slice(g * ROWS, (g + 1) * ROWS)
                     nc.tensor.matmul_mx(
                         out=s_bank(i, g)[:, r],
@@ -189,6 +208,10 @@ def tile_rows_a_relu_mask_kernel(tc, qT, kT, t, v, mask, out):
                 store(i, 0, 2)
                 store(i, 2, 2)
 
+        nc.vector.memset(z_bf[:], 0.0)
+        nc.scalar.activation(out=z_act[:], in_=z_bf[:, 0:1], func=ACT.Relu)
+        quantize(z_codes[:], z_scales[:], z_bf[:])
+        keep_warm(WARM_HEAD)
         k_in = k_raw[:].rearrange("p j (s r) -> p s j r", r=PACK)
         k_out = k_bf[:].rearrange("p r s j -> p s j r")
         nc.vector.tensor_copy(out=k_out[:, :, :, 0:3], in_=k_in[:, :, :, 0:3])
@@ -196,7 +219,8 @@ def tile_rows_a_relu_mask_kernel(tc, qT, kT, t, v, mask, out):
         interleave_q(0)
         quantize(k_codes[:], k_scales[:], k_bf[:].rearrange("p r s j -> p (r s j)"))
         quantize_q(0)
-        scores(0)
+        scores(0, (0, 3, 1, 2))
+        keep_warm(8)
         nc.vector.tensor_tensor(
             out=mt[0][:].rearrange("p (c i) r -> p c r i", i=2),
             in0=m_raw[0][:].rearrange("p r (c i) -> p c r i", i=2),
@@ -210,7 +234,8 @@ def tile_rows_a_relu_mask_kernel(tc, qT, kT, t, v, mask, out):
         for g in range(3):
             weights_vector(0, g)
         quantize_q(1, 2)
-        scores(1)
+        scores(1, (0, 3, 1, 2))
+        keep_warm(4)
         quantize_w(0)
         scale_mask(1)
         interleave_mask(1)
@@ -220,24 +245,35 @@ def tile_rows_a_relu_mask_kernel(tc, qT, kT, t, v, mask, out):
             interleave(v_bf[:, k], v_raw[:, k])
 
         def step(i, pe_before, scalar_before, pe_after, scalar_after):
+            more = i + 1 < GROUPS
             weights_gpsimd(i)
-            weights_vector(i, 0)
             for work in pe_before:
                 work()
-            if i + 1 < GROUPS:
-                scores(i + 1)
+            if more:
+                if not pe_before:
+                    keep_warm(4)
+                scores(i + 1, (3, 0))
+                keep_warm(2)
+            weights_vector(i, 0)
             if i + 2 < GROUPS:
                 interleave_q(i + 2)
             for work in scalar_before:
                 work()
-            if i + 1 < GROUPS:
+            if more:
                 relu_scalar(i + 1)
+            weights_vector(i, 1)
+            if more:
+                scores(i + 1, (1,))
             for work in pe_after:
                 work()
+            if not pe_after:
+                keep_warm(3)
             for work in scalar_after:
                 work()
-            weights_vector(i, 1)
             weights_vector(i, 2)
+            if more:
+                scores(i + 1, (2,))
+            keep_warm(2)
             if i + 2 < GROUPS:
                 quantize_q(i + 2)
             if i == 2:

@@ -54,10 +54,9 @@ def tile_rows_a_relu_mask_kernel(tc, qT, kT, t, v, mask, out):
         w_bf = tile("w_bf", [P, TILES, QT, PACK], BF16)
         w_codes = tile("w_codes", [P, GROUPS, TILES * QT], U32)
         w_scales = tile("w_scales", [P, GROUPS, TILES * QT], U8)
-        p_f32 = [tile("p_f32_%d" % n, [P, QT, PACK], F32) for n in range(2)]
         y_sb = [tile("y_sb%d" % i, [P, TILES, D], F32) for i in range(GROUPS)]
 
-        nbanks = (2, 1, 1, 1)
+        nbanks = (1, 1, 1, 1)
         s_banks = [[ps.tile([P, PACK, QT], F32, name="s%d%d" % (g, n)) for n in range(nbanks[g])] for g in range(TILES)]
         y_banks = [ps.tile([P, TILES, D], F32, name="y%d" % n) for n in range(2)]
 
@@ -143,9 +142,9 @@ def tile_rows_a_relu_mask_kernel(tc, qT, kT, t, v, mask, out):
 
         def scores(i, tiles):
             cols = slice(i * QT, (i + 1) * QT)
-            for g in tiles:
-                for r in range(PACK):
-                    keys = slice(r * P, (r + 1) * P)
+            for r in range(PACK):
+                keys = slice(r * P, (r + 1) * P)
+                for g in tiles:
                     rows = slice(g * ROWS, (g + 1) * ROWS)
                     nc.tensor.matmul_mx(
                         out=s_bank(i, g)[:, r],
@@ -167,16 +166,9 @@ def tile_rows_a_relu_mask_kernel(tc, qT, kT, t, v, mask, out):
                 op1=ALU.mult,
             )
 
-        def relu_scalar(i):
-            nc.scalar.activation(out=p_f32[i % 2][:], in_=s_bank(i, 3)[:].rearrange("p r q -> p q r"), func=ACT.Relu)
-
-        def weights_gpsimd(i):
-            nc.gpsimd.tensor_tensor(out=w_bf[:, 3], in0=p_f32[i % 2][:], in1=mt[i // 2][:], op=ALU.mult)
-
-        def quantize_w(i):
-            for g0 in (0, 2):
-                cols = slice(g0 * QT, (g0 + 2) * QT)
-                quantize(w_codes[:, i, cols], w_scales[:, i, cols], w_bf[:, g0 : g0 + 2].rearrange("p g q r -> p (g q r)"))
+        def quantize_w(i, g0, count):
+            cols = slice(g0 * QT, (g0 + count) * QT)
+            quantize(w_codes[:, i, cols], w_scales[:, i, cols], w_bf[:, g0 : g0 + count].rearrange("p g q r -> p (g q r)"))
 
         def y_bank(i, g):
             return y_banks[(i + (g // 2 if i == GROUPS - 1 else 0)) % 2]
@@ -219,7 +211,8 @@ def tile_rows_a_relu_mask_kernel(tc, qT, kT, t, v, mask, out):
         interleave_q(0)
         quantize(k_codes[:], k_scales[:], k_bf[:].rearrange("p r s j -> p (r s j)"))
         quantize_q(0)
-        scores(0, (0, 3, 1, 2))
+        scores(0, (0, 1))
+        scores(0, (2, 3))
         keep_warm(8)
         nc.vector.tensor_tensor(
             out=mt[0][:].rearrange("p (c i) r -> p c r i", i=2),
@@ -227,69 +220,60 @@ def tile_rows_a_relu_mask_kernel(tc, qT, kT, t, v, mask, out):
             in1=t_sb[:].unsqueeze(1).unsqueeze(3).to_broadcast([P, QT // 2, PACK, 2]),
             op=ALU.mult,
         )
-        relu_scalar(0)
-        weights_gpsimd(0)
         interleave_q(1)
-        interleave_q(2)
-        for g in range(3):
-            weights_vector(0, g)
-        quantize_q(1, 2)
-        scores(1, (0, 3, 1, 2))
-        keep_warm(4)
-        quantize_w(0)
-        scale_mask(1)
-        interleave_mask(1)
-        relu_scalar(1)
-
-        def v_half(k):
-            interleave(v_bf[:, k], v_raw[:, k])
-
-        def step(i, pe_before, scalar_before, pe_after, scalar_after):
-            more = i + 1 < GROUPS
-            weights_gpsimd(i)
-            for work in pe_before:
-                work()
-            if more:
-                if not pe_before:
-                    keep_warm(4)
-                scores(i + 1, (3, 0))
-                keep_warm(2)
+        last = GROUPS - 1
+        for i in range(GROUPS):
             weights_vector(i, 0)
+            if i == 0:
+                quantize_q(1)
+            if i == 2:
+                values(0)
+                values(1)
+            elif i > 2:
+                values(i - 1, (2, 3))
+                keep_warm(4)
+            else:
+                keep_warm(6)
             if i + 2 < GROUPS:
                 interleave_q(i + 2)
-            for work in scalar_before:
-                work()
-            if more:
-                relu_scalar(i + 1)
+            if i == 0:
+                scale_mask(1)
+                interleave_mask(1)
+            if i == 1:
+                for k in range(KV):
+                    interleave(v_bf[:, k], v_raw[:, k])
+            if i == 2:
+                finish(0)
+            if i >= 2:
+                finish(i - 1)
+            if i == 2:
+                scale_mask(2)
+            if i == 3:
+                interleave_mask(2)
+                interleave_mask(3)
             weights_vector(i, 1)
-            if more:
-                scores(i + 1, (1,))
-            for work in pe_after:
-                work()
-            if not pe_after:
+            if i < last:
+                scores(i + 1, (0, 1))
                 keep_warm(3)
-            for work in scalar_after:
-                work()
             weights_vector(i, 2)
-            if more:
-                scores(i + 1, (2,))
-            keep_warm(2)
+            quantize_w(i, 0, 2)
+            if i >= 2:
+                values(i, (0, 1))
+            else:
+                keep_warm(3)
+            weights_vector(i, 3)
+            if i < last:
+                scores(i + 1, (2, 3))
             if i + 2 < GROUPS:
                 quantize_q(i + 2)
-            if i == 2:
+            if i == 1:
                 quantize(v_codes[:], v_scales[:], v_bf[:].rearrange("p k e r -> p (k e r)"))
-            quantize_w(i)
-
-        step(1, [], [], [], [lambda: v_half(0), lambda: v_half(1)])
-        step(2, [], [], [], [lambda: scale_mask(2)])
-        step(3, [lambda: values(0), lambda: values(1)], [lambda: finish(0)], [lambda: values(2)], [lambda: interleave_mask(2)])
-        step(4, [], [lambda: finish(1)], [lambda: values(3)], [lambda: finish(2)])
-        step(5, [lambda: values(4)], [lambda: finish(3)], [], [lambda: interleave_mask(3)])
-        step(6, [lambda: values(5)], [lambda: finish(4)], [], [lambda: finish(5)])
-        step(7, [lambda: values(6)], [lambda: finish(6)], [], [])
-        last = GROUPS - 1
-        values(last)
+            if i < last:
+                quantize_w(i, 2, 2)
         nc.scalar.activation(out=y_sb[last][:, 0:2], in_=y_bank(last, 0)[:, 0:2], func=ACT.Copy, scale=OUT_SCALE)
         store(last, 0, 2)
-        nc.vector.tensor_scalar_mul(y_sb[last][:, 2:4], y_bank(last, 2)[:, 2:4], OUT_SCALE)
+        for g in (2, 3):
+            quantize_w(last, g, 1)
+        values(last, (2, 3))
+        nc.scalar.activation(out=y_sb[last][:, 2:4], in_=y_bank(last, 2)[:, 2:4], func=ACT.Copy, scale=OUT_SCALE)
         store(last, 2, 2)

@@ -21,7 +21,6 @@ QT = 128
 GROUPS = 8
 SETS = ((2, 3, 4, 5), (0, 1, 6, 7))
 OUT_SCALE = 1.0 / 16.0
-WARM_HEAD = 48
 
 
 def tile_rows_a_relu_mask_kernel(tc, qT, kT, t, v, mask, out):
@@ -54,29 +53,15 @@ def tile_rows_a_relu_mask_kernel(tc, qT, kT, t, v, mask, out):
         w_bf = tile("w_bf", [P, TILES, QT, PACK], BF16)
         w_codes = tile("w_codes", [P, GROUPS, TILES * QT], U32)
         w_scales = tile("w_scales", [P, GROUPS, TILES * QT], U8)
+        p_f32 = [tile("p_f32_%d" % n, [P, QT, PACK], F32) for n in range(2)]
         y_sb = [tile("y_sb%d" % i, [P, TILES, D], F32) for i in range(GROUPS)]
 
-        nbanks = (1, 1, 1, 1)
+        nbanks = (1, 2, 2, 1)
         s_banks = [[ps.tile([P, PACK, QT], F32, name="s%d%d" % (g, n)) for n in range(nbanks[g])] for g in range(TILES)]
         y_banks = [ps.tile([P, TILES, D], F32, name="y%d" % n) for n in range(2)]
 
-        spare_bank = ps.tile([P, TILES, D], F32, name="spare")
-        z_bf = tile("z_bf", [P, 512], BF16)
-        z_codes = tile("z_codes", [P, P], U32)
-        z_scales = tile("z_scales", [P, P], U8)
+        z_in = tile("z_in", [P, 1], F32)
         z_act = tile("z_act", [P, 1], F32)
-
-        def keep_warm(count):
-            for n in range(count):
-                nc.tensor.matmul_mx(
-                    out=spare_bank[:, n % TILES],
-                    lhsT=z_codes[:].bitcast(FP8X4),
-                    lhsT_scale=z_scales[:],
-                    rhs=z_codes[:].bitcast(FP8X4),
-                    rhs_scale=z_scales[:],
-                    start=True,
-                    stop=True,
-                )
 
         def s_bank(i, g):
             return s_banks[g][i % nbanks[g]]
@@ -98,16 +83,18 @@ def tile_rows_a_relu_mask_kernel(tc, qT, kT, t, v, mask, out):
             c0, w = chunks[n]
             nc.sync.dma_start(out=m_raw[n][:], in_=mask[:, c0 : c0 + w].rearrange("(p r) q -> p r q", r=PACK))
 
-        for g, queue in ((0, nc.sync), (2, nc.scalar), (1, nc.sync), (3, nc.scalar)):
-            queue.dma_start(out=k_raw[g * ROWS : (g + 1) * ROWS], in_=kT[g // 2].rearrange("(p j) n -> p j n", j=PACK))
+        k_rows = kT.rearrange("k (p j) n -> (k p) j n", j=PACK)
+        nc.sync.dma_start(out=k_raw[ROWS : 3 * ROWS], in_=k_rows)
+        nc.scalar.dma_start(out=k_raw[3 * ROWS :], in_=k_rows[ROWS:])
+        nc.sync.dma_start(out=k_raw[:ROWS], in_=k_rows[:ROWS])
         nc.scalar.dma_start(out=t_sb[:], in_=t.rearrange("(p r) o -> p (r o)", r=PACK))
         load_q(0, 0)
         load_mask(0)
         load_q(1, 0)
         load_q(0, 1)
         load_mask(1)
-        load_q(1, 1)
         nc.sync.dma_start(out=v_raw[:], in_=v.rearrange("k (p r) e -> p k r e", r=PACK))
+        load_q(1, 1)
         load_q(0, 2)
         load_mask(2)
         load_q(1, 2)
@@ -129,9 +116,9 @@ def tile_rows_a_relu_mask_kernel(tc, qT, kT, t, v, mask, out):
             cols = slice(i * QT, (i + count) * QT)
             quantize(q_codes[:, cols], q_scales[:, cols], q_bf[:, i : i + count].rearrange("p g q j -> p (g q j)"))
 
-        def scale_mask(n):
+        def scale_mask(c):
             for r in range(PACK):
-                nc.scalar.activation(out=m_scaled[n][:, r], in_=m_raw[n][:, r], func=ACT.Copy, scale=t_sb[:, r : r + 1])
+                nc.scalar.activation(out=window(m_scaled, c)[:, r], in_=window(m_raw, c)[:, r], func=ACT.Copy, scale=t_sb[:, r : r + 1])
 
         def interleave_mask(c):
             nc.scalar.activation(
@@ -165,6 +152,12 @@ def tile_rows_a_relu_mask_kernel(tc, qT, kT, t, v, mask, out):
                 op0=ALU.max,
                 op1=ALU.mult,
             )
+
+        def relu_scalar(i):
+            nc.scalar.activation(out=p_f32[i % 2][:], in_=s_bank(i, 3)[:].rearrange("p r q -> p q r"), func=ACT.Relu)
+
+        def weights_gpsimd(i):
+            nc.gpsimd.tensor_tensor(out=w_bf[:, 3], in0=p_f32[i % 2][:], in1=mt[i // 2][:], op=ALU.mult)
 
         def quantize_w(i, g0, count):
             cols = slice(g0 * QT, (g0 + count) * QT)
@@ -200,20 +193,24 @@ def tile_rows_a_relu_mask_kernel(tc, qT, kT, t, v, mask, out):
                 store(i, 0, 2)
                 store(i, 2, 2)
 
-        nc.vector.memset(z_bf[:], 0.0)
-        nc.scalar.activation(out=z_act[:], in_=z_bf[:, 0:1], func=ACT.Relu)
-        quantize(z_codes[:], z_scales[:], z_bf[:])
-        keep_warm(WARM_HEAD)
+        nc.vector.memset(z_in[:], 0.0)
+        nc.scalar.activation(out=z_act[:], in_=z_in[:], func=ACT.Relu)
         k_in = k_raw[:].rearrange("p j (s r) -> p s j r", r=PACK)
         k_out = k_bf[:].rearrange("p r s j -> p s j r")
-        nc.vector.tensor_copy(out=k_out[:, :, :, 0:3], in_=k_in[:, :, :, 0:3])
-        nc.scalar.activation(out=k_bf[:, 3], in_=k_in[:, :, :, 3], func=ACT.Copy)
-        interleave_q(0)
-        quantize(k_codes[:], k_scales[:], k_bf[:].rearrange("p r s j -> p (r s j)"))
+        nc.vector.tensor_copy(out=k_out[:, :, :, 0:2], in_=k_in[:, :, :, 0:2])
+        nc.scalar.activation(out=k_out[:, :, :, 2:4], in_=k_in[:, :, :, 2:4], func=ACT.Copy)
+        nc.vector.tensor_copy(
+            out=q_bf[:, 0].rearrange("p (c i) j -> p c j i", i=4),
+            in_=q_raw[0][0][:].rearrange("p j (c i) -> p c j i", i=4),
+        )
+
+        def quantize_k(r0):
+            cols = slice(r0 * P, (r0 + 2) * P)
+            quantize(k_codes[:, cols], k_scales[:, cols], k_bf[:, r0 : r0 + 2].rearrange("p r s j -> p (r s j)"))
+
+        quantize_k(0)
         quantize_q(0)
-        scores(0, (0, 1))
-        scores(0, (2, 3))
-        keep_warm(8)
+        quantize_k(2)
         nc.vector.tensor_tensor(
             out=mt[0][:].rearrange("p (c i) r -> p c r i", i=2),
             in0=m_raw[0][:].rearrange("p r (c i) -> p c r i", i=2),
@@ -221,59 +218,47 @@ def tile_rows_a_relu_mask_kernel(tc, qT, kT, t, v, mask, out):
             op=ALU.mult,
         )
         interleave_q(1)
+        quantize_q(1)
         last = GROUPS - 1
         for i in range(GROUPS):
-            weights_vector(i, 0)
-            if i == 0:
-                quantize_q(1)
-            if i == 2:
-                values(0)
-                values(1)
-            elif i > 2:
-                values(i - 1, (2, 3))
-                keep_warm(4)
-            else:
-                keep_warm(6)
-            if i + 2 < GROUPS:
-                interleave_q(i + 2)
-            if i == 0:
-                scale_mask(1)
-                interleave_mask(1)
+            scores(i, (3, 0))
+            scores(i, (1, 2))
+            if i in (3, 5, 7):
+                finish(i - 3)
+            relu_scalar(i)
+            weights_gpsimd(i)
+            if i in (1, 3):
+                interleave_mask(i // 2 + 1)
             if i == 1:
                 for k in range(KV):
                     interleave(v_bf[:, k], v_raw[:, k])
-            if i == 2:
-                finish(0)
-            if i >= 2:
-                finish(i - 1)
-            if i == 2:
-                scale_mask(2)
-            if i == 3:
-                interleave_mask(2)
+            if i + 2 < GROUPS:
+                interleave_q(i + 2)
+            if i in (0, 2, 4):
+                scale_mask(i // 2 + 1)
+            if i == 5:
                 interleave_mask(3)
-            weights_vector(i, 1)
-            if i < last:
-                scores(i + 1, (0, 1))
-                keep_warm(3)
-            weights_vector(i, 2)
-            quantize_w(i, 0, 2)
-            if i >= 2:
-                values(i, (0, 1))
-            else:
-                keep_warm(3)
-            weights_vector(i, 3)
-            if i < last:
-                scores(i + 1, (2, 3))
+            if i in (3, 5, 7):
+                finish(i - 2)
+            for g in range(3):
+                weights_vector(i, g)
+            if i in (2, 4, 6):
+                values(i - 2)
+            if i in (2, 4, 6, 7):
+                values(i - 1)
             if i + 2 < GROUPS:
                 quantize_q(i + 2)
             if i == 1:
                 quantize(v_codes[:], v_scales[:], v_bf[:].rearrange("p k e r -> p (k e r)"))
+            quantize_w(i, 0, 2)
             if i < last:
                 quantize_w(i, 2, 2)
+        finish(last - 1)
+        values(last, (0, 1))
         nc.scalar.activation(out=y_sb[last][:, 0:2], in_=y_bank(last, 0)[:, 0:2], func=ACT.Copy, scale=OUT_SCALE)
         store(last, 0, 2)
-        for g in (2, 3):
+        for g in (3, 2):
             quantize_w(last, g, 1)
-        values(last, (2, 3))
-        nc.scalar.activation(out=y_sb[last][:, 2:4], in_=y_bank(last, 2)[:, 2:4], func=ACT.Copy, scale=OUT_SCALE)
+        values(last, (3, 2))
+        nc.vector.tensor_scalar_mul(y_sb[last][:, 2:4], y_bank(last, 2)[:, 2:4], OUT_SCALE)
         store(last, 2, 2)

@@ -15,11 +15,18 @@ ALU = mybir.AluOpType
 
 P = 128
 PACK = 4
-ROWS = 32
-TILES = 4
+ROWS = D // PACK
+TILES = P // ROWS
 QT = 128
-GROUPS = 8
+BLOCKS = NQ // QT
 SETS = ((2, 3, 4, 5), (0, 1, 6, 7))
+HEAD_RUNS = (((0, 4),), ((0, 2), (2, 2)))
+LOADS = ((0, 1), (1, 1), (2, 2))
+GROUPS = len(SETS) * BLOCKS
+SCORE_BANKS = (1, 2, 2, 1)
+VECTOR_TILES = (0, 1, 2)
+SHARED_TILE = 3
+Y_BANKS = 2
 OUT_SCALE = 1.0 / 16.0
 
 
@@ -33,140 +40,140 @@ def tile_rows_a_relu_mask_kernel(tc, qT, kT, t, v, mask, out):
         def tile(name, shape, dtype):
             return sb.tile(shape, dtype, name=name, align_bytes=64)
 
-        chunks = ((0, 128), (128, 128), (256, 256))
         k_raw = tile("k_raw", [P, PACK, N], F32)
         t_sb = tile("t_sb", [P, PACK], F32)
         v_raw = tile("v_raw", [P, KV, PACK, D], F32)
-        q_raw = [[tile("q_raw%d%d" % (s, n), [P, PACK, w], F32) for n, (c0, w) in enumerate(chunks)] for s in range(2)]
-        m_raw = [tile("m_raw%d" % n, [P, PACK, w], F32) for n, (c0, w) in enumerate(chunks)]
-        m_scaled = [tile("m_scaled%d" % n, [P, PACK, w], F32) for n, (c0, w) in enumerate(chunks)]
-        mt = [tile("mt%d" % c, [P, QT, PACK], F32) for c in range(4)]
+        q_raw = [
+            [tile("q_raw%d%d" % (s, c0), [P, PACK, count * QT], F32) for c0, count in LOADS] for s in range(len(SETS))
+        ]
+        mask_raw = [tile("mask_raw%d" % c0, [P, PACK, count * QT], F32) for c0, count in LOADS]
+        mask_t_rows = {c: tile("mask_t_rows%d" % c, [P, PACK, QT], F32) for c in range(1, BLOCKS)}
+        mask_t = [tile("mask_t%d" % c, [P, QT, PACK], F32) for c in range(BLOCKS)]
         k_bf = tile("k_bf", [P, PACK, P, PACK], BF16)
         k_codes = tile("k_codes", [P, N], U32)
         k_scales = tile("k_scales", [P, N], U8)
         q_bf = tile("q_bf", [P, GROUPS, QT, PACK], BF16)
-        q_codes = tile("q_codes", [P, GROUPS * QT], U32)
-        q_scales = tile("q_scales", [P, GROUPS * QT], U8)
+        q_codes = tile("q_codes", [P, GROUPS, QT], U32)
+        q_scales = tile("q_scales", [P, GROUPS, QT], U8)
         v_bf = tile("v_bf", [P, KV, D, PACK], BF16)
         v_codes = tile("v_codes", [P, KV * D], U32)
         v_scales = tile("v_scales", [P, KV * D], U8)
         w_bf = tile("w_bf", [P, TILES, QT, PACK], BF16)
         w_codes = tile("w_codes", [P, GROUPS, TILES * QT], U32)
         w_scales = tile("w_scales", [P, GROUPS, TILES * QT], U8)
-        p_f32 = [tile("p_f32_%d" % n, [P, QT, PACK], F32) for n in range(2)]
+        relu_sb = [tile("relu_sb%d" % n, [P, QT, PACK], F32) for n in range(2)]
         y_sb = [tile("y_sb%d" % i, [P, TILES, D], F32) for i in range(GROUPS)]
+        table_in = tile("table_in", [P, 1], F32)
+        table_out = tile("table_out", [P, 1], F32)
+        score_banks = [
+            [ps.tile([P, PACK, QT], F32, name="s%d%d" % (g, n)) for n in range(count)]
+            for g, count in enumerate(SCORE_BANKS)
+        ]
+        y_banks = [ps.tile([P, TILES, D], F32, name="y%d" % n) for n in range(Y_BANKS)]
+        last = GROUPS - 1
 
-        nbanks = (1, 2, 2, 1)
-        s_banks = [[ps.tile([P, PACK, QT], F32, name="s%d%d" % (g, n)) for n in range(nbanks[g])] for g in range(TILES)]
-        y_banks = [ps.tile([P, TILES, D], F32, name="y%d" % n) for n in range(2)]
-
-        z_in = tile("z_in", [P, 1], F32)
-        z_act = tile("z_act", [P, 1], F32)
-
-        def s_bank(i, g):
-            return s_banks[g][i % nbanks[g]]
-
-        def window(tiles, c):
-            n = min(c, 2)
-            lo = c * QT - chunks[n][0]
-            return tiles[n][:, :, lo : lo + QT]
+        def load_columns(n):
+            c0, count = LOADS[n]
+            return slice(c0 * QT, (c0 + count) * QT)
 
         def load_q(s, n):
-            c0, w = chunks[n]
-            heads = SETS[s]
-            runs = ((0, 4),) if s == 0 else ((0, 2), (2, 2))
-            for g0, count in runs:
-                src = qT[heads[g0] : heads[g0] + count, :, c0 : c0 + w].rearrange("h (p j) q -> (h p) j q", j=PACK)
+            for g0, count in HEAD_RUNS[s]:
+                h0 = SETS[s][g0]
+                src = qT[h0 : h0 + count, :, load_columns(n)].rearrange("h (p j) q -> (h p) j q", j=PACK)
                 nc.sync.dma_start(out=q_raw[s][n][g0 * ROWS : (g0 + count) * ROWS], in_=src)
 
         def load_mask(n):
-            c0, w = chunks[n]
-            nc.sync.dma_start(out=m_raw[n][:], in_=mask[:, c0 : c0 + w].rearrange("(p r) q -> p r q", r=PACK))
+            src = mask[:, load_columns(n)].rearrange("(p r) q -> p r q", r=PACK)
+            nc.sync.dma_start(out=mask_raw[n][:], in_=src)
+
+        def block(tiles, c):
+            n = min(c, len(LOADS) - 1)
+            lo = (c - LOADS[n][0]) * QT
+            return tiles[n][:, :, lo : lo + QT]
 
         k_rows = kT.rearrange("k (p j) n -> (k p) j n", j=PACK)
-        nc.sync.dma_start(out=k_raw[ROWS : 3 * ROWS], in_=k_rows)
-        nc.scalar.dma_start(out=k_raw[3 * ROWS :], in_=k_rows[ROWS:])
         nc.sync.dma_start(out=k_raw[:ROWS], in_=k_rows[:ROWS])
+        nc.scalar.dma_start(out=k_raw[3 * ROWS :], in_=k_rows[ROWS:])
+        nc.sync.dma_start(out=k_raw[ROWS : 3 * ROWS], in_=k_rows)
         nc.scalar.dma_start(out=t_sb[:], in_=t.rearrange("(p r) o -> p (r o)", r=PACK))
-        load_q(0, 0)
-        load_mask(0)
-        load_q(1, 0)
-        load_q(0, 1)
-        load_mask(1)
-        nc.sync.dma_start(out=v_raw[:], in_=v.rearrange("k (p r) e -> p k r e", r=PACK))
-        load_q(1, 1)
-        load_q(0, 2)
-        load_mask(2)
-        load_q(1, 2)
+        for n in range(len(LOADS)):
+            load_q(0, n)
+            load_mask(n)
+            load_q(1, n)
+            if n == 1:
+                nc.sync.dma_start(out=v_raw[:], in_=v.rearrange("k (p r) e -> p k r e", r=PACK))
 
         def quantize(codes, scales, src):
             nc.vector.quantize_mx(out=codes.bitcast(FP8X4), scales=scales, in_=src)
 
         def interleave(dst, src):
-            nc.scalar.activation(
-                out=dst.rearrange("p (c i) j -> p c j i", i=4),
-                in_=src.rearrange("p j (c i) -> p c j i", i=4),
-                func=ACT.Copy,
-            )
+            nc.scalar.activation(out=dst, in_=src.rearrange("p j c -> p c j"), func=ACT.Copy)
 
         def interleave_q(i):
-            interleave(q_bf[:, i], window(q_raw[i % 2], i // 2))
+            interleave(q_bf[:, i], block(q_raw[i % 2], i // 2))
 
-        def quantize_q(i, count=1):
-            cols = slice(i * QT, (i + count) * QT)
-            quantize(q_codes[:, cols], q_scales[:, cols], q_bf[:, i : i + count].rearrange("p g q j -> p (g q j)"))
+        def quantize_q(i):
+            quantize(q_codes[:, i], q_scales[:, i], q_bf[:, i].rearrange("p q j -> p (q j)"))
+
+        def quantize_k(r0):
+            cols = slice(r0 * P, (r0 + 2) * P)
+            quantize(k_codes[:, cols], k_scales[:, cols], k_bf[:, r0 : r0 + 2].rearrange("p r s j -> p (r s j)"))
 
         def scale_mask(c):
             for r in range(PACK):
-                nc.scalar.activation(out=window(m_scaled, c)[:, r], in_=window(m_raw, c)[:, r], func=ACT.Copy, scale=t_sb[:, r : r + 1])
+                nc.scalar.activation(
+                    out=mask_t_rows[c][:, r], in_=block(mask_raw, c)[:, r], func=ACT.Copy, scale=t_sb[:, r : r + 1]
+                )
 
         def interleave_mask(c):
-            nc.scalar.activation(
-                out=mt[c][:].rearrange("p (c i) r -> p c r i", i=2),
-                in_=window(m_scaled, c).rearrange("p r (c i) -> p c r i", i=2),
-                func=ACT.Copy,
-            )
+            interleave(mask_t[c][:], mask_t_rows[c][:])
+
+        def interleave_v(k):
+            interleave(v_bf[:, k], v_raw[:, k])
+
+        def score_bank(i, g):
+            return score_banks[g][i % SCORE_BANKS[g]]
 
         def scores(i, tiles):
-            cols = slice(i * QT, (i + 1) * QT)
             for r in range(PACK):
                 keys = slice(r * P, (r + 1) * P)
                 for g in tiles:
                     rows = slice(g * ROWS, (g + 1) * ROWS)
                     nc.tensor.matmul_mx(
-                        out=s_bank(i, g)[:, r],
+                        out=score_bank(i, g)[:, r],
                         lhsT=k_codes[rows, keys].bitcast(FP8X4),
                         lhsT_scale=k_scales[rows, keys],
-                        rhs=q_codes[rows, cols].bitcast(FP8X4),
-                        rhs_scale=q_scales[rows, cols],
+                        rhs=q_codes[rows, i].bitcast(FP8X4),
+                        rhs_scale=q_scales[rows, i],
                         start=True,
                         stop=True,
                     )
 
-        def weights_vector(i, g):
+        def weights(i, g):
             nc.vector.scalar_tensor_tensor(
                 out=w_bf[:, g],
-                in0=s_bank(i, g)[:].rearrange("p r q -> p q r"),
+                in0=score_bank(i, g)[:].rearrange("p r q -> p q r"),
                 scalar=0.0,
-                in1=mt[i // 2][:],
+                in1=mask_t[i // 2][:],
                 op0=ALU.max,
                 op1=ALU.mult,
             )
 
-        def relu_scalar(i):
-            nc.scalar.activation(out=p_f32[i % 2][:], in_=s_bank(i, 3)[:].rearrange("p r q -> p q r"), func=ACT.Relu)
-
-        def weights_gpsimd(i):
-            nc.gpsimd.tensor_tensor(out=w_bf[:, 3], in0=p_f32[i % 2][:], in1=mt[i // 2][:], op=ALU.mult)
+        def shared_weights(i):
+            relu = relu_sb[i % 2]
+            src = score_bank(i, SHARED_TILE)[:].rearrange("p r q -> p q r")
+            nc.scalar.activation(out=relu[:], in_=src, func=ACT.Relu)
+            nc.gpsimd.tensor_tensor(out=w_bf[:, SHARED_TILE], in0=relu[:], in1=mask_t[i // 2][:], op=ALU.mult)
 
         def quantize_w(i, g0, count):
             cols = slice(g0 * QT, (g0 + count) * QT)
-            quantize(w_codes[:, i, cols], w_scales[:, i, cols], w_bf[:, g0 : g0 + count].rearrange("p g q r -> p (g q r)"))
+            src = w_bf[:, g0 : g0 + count].rearrange("p g q r -> p (g q r)")
+            quantize(w_codes[:, i, cols], w_scales[:, i, cols], src)
 
         def y_bank(i, g):
-            return y_banks[(i + (g // 2 if i == GROUPS - 1 else 0)) % 2]
+            return y_banks[(i + (g // 2 if i == last else 0)) % Y_BANKS]
 
-        def values(i, tiles=range(TILES)):
+        def values(i, tiles):
             for g in tiles:
                 cols = slice(g * QT, (g + 1) * QT)
                 feats = slice(g // 2 * D, (g // 2 + 1) * D)
@@ -183,76 +190,69 @@ def tile_rows_a_relu_mask_kernel(tc, qT, kT, t, v, mask, out):
         def store(i, g0, count):
             h0 = SETS[i % 2][g0]
             rows = slice(i // 2 * QT, (i // 2 + 1) * QT)
-            nc.sync.dma_start(out=out[h0 : h0 + count, rows, :].rearrange("h q e -> q h e"), in_=y_sb[i][:, g0 : g0 + count])
+            dst = out[h0 : h0 + count, rows, :].rearrange("h q e -> q h e")
+            nc.sync.dma_start(out=dst, in_=y_sb[i][:, g0 : g0 + count])
 
         def finish(i):
             nc.scalar.activation(out=y_sb[i][:], in_=y_bank(i, 0)[:], func=ACT.Copy, scale=OUT_SCALE)
-            if i % 2 == 0:
-                store(i, 0, 4)
-            else:
-                store(i, 0, 2)
-                store(i, 2, 2)
+            for g0, count in HEAD_RUNS[i % 2]:
+                store(i, g0, count)
 
-        nc.vector.memset(z_in[:], 0.0)
-        nc.scalar.activation(out=z_act[:], in_=z_in[:], func=ACT.Relu)
+        nc.vector.memset(table_in[:], 0.0)
+        nc.scalar.activation(out=table_out[:], in_=table_in[:], func=ACT.Relu)
+
         k_in = k_raw[:].rearrange("p j (s r) -> p s j r", r=PACK)
         k_out = k_bf[:].rearrange("p r s j -> p s j r")
         nc.vector.tensor_copy(out=k_out[:, :, :, 0:2], in_=k_in[:, :, :, 0:2])
         nc.scalar.activation(out=k_out[:, :, :, 2:4], in_=k_in[:, :, :, 2:4], func=ACT.Copy)
-        nc.vector.tensor_copy(
-            out=q_bf[:, 0].rearrange("p (c i) j -> p c j i", i=4),
-            in_=q_raw[0][0][:].rearrange("p j (c i) -> p c j i", i=4),
-        )
-
-        def quantize_k(r0):
-            cols = slice(r0 * P, (r0 + 2) * P)
-            quantize(k_codes[:, cols], k_scales[:, cols], k_bf[:, r0 : r0 + 2].rearrange("p r s j -> p (r s j)"))
-
+        nc.vector.tensor_copy(out=q_bf[:, 0], in_=q_raw[0][0][:].rearrange("p j q -> p q j"))
         quantize_k(0)
         quantize_q(0)
         quantize_k(2)
         nc.vector.tensor_tensor(
-            out=mt[0][:].rearrange("p (c i) r -> p c r i", i=2),
-            in0=m_raw[0][:].rearrange("p r (c i) -> p c r i", i=2),
-            in1=t_sb[:].unsqueeze(1).unsqueeze(3).to_broadcast([P, QT // 2, PACK, 2]),
+            out=mask_t[0][:],
+            in0=mask_raw[0][:].rearrange("p r q -> p q r"),
+            in1=t_sb[:].unsqueeze(1).to_broadcast([P, QT, PACK]),
             op=ALU.mult,
         )
         interleave_q(1)
-        quantize_q(1)
-        last = GROUPS - 1
+
+        values_after_scores = {3: (0, 1), 5: (2, 3), 6: (4, 5), 7: (6,)}
+        finish_pair = {step + 1: groups for step, groups in values_after_scores.items() if len(groups) == 2}
+        scale_mask_in = {0: 1, 2: 2, 3: 3}
+        interleave_mask_in = {1: 1, 3: 2, 5: 3}
+        interleave_v_in = {1: 0, 2: 1}
+        quantize_v_in = 2
         for i in range(GROUPS):
-            scores(i, (3, 0))
+            scores(i, (SHARED_TILE, 0))
             scores(i, (1, 2))
-            if i in (3, 5, 7):
-                finish(i - 3)
-            relu_scalar(i)
-            weights_gpsimd(i)
-            if i in (1, 3):
-                interleave_mask(i // 2 + 1)
-            if i == 1:
-                for k in range(KV):
-                    interleave(v_bf[:, k], v_raw[:, k])
+            if i in finish_pair:
+                finish(finish_pair[i][0])
+            shared_weights(i)
+            if i in interleave_mask_in:
+                interleave_mask(interleave_mask_in[i])
             if i + 2 < GROUPS:
                 interleave_q(i + 2)
-            if i in (0, 2, 4):
-                scale_mask(i // 2 + 1)
-            if i == 5:
-                interleave_mask(3)
-            if i in (3, 5, 7):
-                finish(i - 2)
-            for g in range(3):
-                weights_vector(i, g)
-            if i in (2, 4, 6):
-                values(i - 2)
-            if i in (2, 4, 6, 7):
-                values(i - 1)
+            if i in interleave_v_in:
+                interleave_v(interleave_v_in[i])
+            if i in scale_mask_in:
+                scale_mask(scale_mask_in[i])
+            if i in finish_pair:
+                finish(finish_pair[i][1])
+            for done in values_after_scores.get(i, ()):
+                values(done, range(TILES))
+            for g in VECTOR_TILES:
+                weights(i, g)
+                if i == 0 and g == 0:
+                    quantize_q(1)
             if i + 2 < GROUPS:
                 quantize_q(i + 2)
-            if i == 1:
+            if i == quantize_v_in:
                 quantize(v_codes[:], v_scales[:], v_bf[:].rearrange("p k e r -> p (k e r)"))
             quantize_w(i, 0, 2)
             if i < last:
                 quantize_w(i, 2, 2)
+
         finish(last - 1)
         values(last, (0, 1))
         nc.scalar.activation(out=y_sb[last][:, 0:2], in_=y_bank(last, 0)[:, 0:2], func=ACT.Copy, scale=OUT_SCALE)

from contextlib import ExitStack

import concourse.mybir as mybir

H, KV, D, NQ, N = 8, 2, 128, 512, 512
FLOPS = 2 * 2 * H * NQ * N * D

F32 = mybir.dt.float32
BF16 = mybir.dt.bfloat16
U32 = mybir.dt.uint32
U8 = mybir.dt.uint8
FP8X4 = mybir.dt.float8_e4m3fn_x4
ACT = mybir.ActivationFunctionType
ALU = mybir.AluOpType

P = 128
PACK = 4
ROWS = D // PACK
TILES = P // ROWS
QT = 128
BLOCKS = NQ // QT
SETS = ((2, 3, 4, 5), (0, 1, 6, 7))
HEAD_RUNS = (((0, 4),), ((0, 2), (2, 2)))
LOADS = ((0, 1), (1, 1), (2, 2))
GROUPS = len(SETS) * BLOCKS
SCORE_BANKS = (1, 2, 2, 1)
VECTOR_TILES = (0, 1, 2)
SHARED_TILE = 3
Y_BANKS = 2
OUT_SCALE = 1.0 / 16.0


def tile_rows_a_relu_mask_kernel(tc, qT, kT, t, v, mask, out):
    nc = tc.nc
    with ExitStack() as ctx:
        sb = ctx.enter_context(tc.tile_pool(name="sb", bufs=1))
        ps = ctx.enter_context(tc.psum_pool(name="ps", bufs=1))
        ctx.enter_context(tc.manual_schedule())

        def tile(name, shape, dtype):
            return sb.tile(shape, dtype, name=name, align_bytes=64)

        k_raw = tile("k_raw", [P, PACK, N], F32)
        t_sb = tile("t_sb", [P, PACK], F32)
        v_raw = tile("v_raw", [P, KV, PACK, D], F32)
        q_raw = [
            [tile("q_raw%d%d" % (s, c0), [P, PACK, count * QT], F32) for c0, count in LOADS] for s in range(len(SETS))
        ]
        mask_raw = [tile("mask_raw%d" % c0, [P, PACK, count * QT], F32) for c0, count in LOADS]
        mask_t_rows = {c: tile("mask_t_rows%d" % c, [P, PACK, QT], F32) for c in range(1, BLOCKS)}
        mask_t = [tile("mask_t%d" % c, [P, QT, PACK], F32) for c in range(BLOCKS)]
        k_bf = tile("k_bf", [P, PACK, P, PACK], BF16)
        k_codes = tile("k_codes", [P, N], U32)
        k_scales = tile("k_scales", [P, N], U8)
        q_bf = tile("q_bf", [P, GROUPS, QT, PACK], BF16)
        q_codes = tile("q_codes", [P, GROUPS, QT], U32)
        q_scales = tile("q_scales", [P, GROUPS, QT], U8)
        v_bf = tile("v_bf", [P, KV, D, PACK], BF16)
        v_codes = tile("v_codes", [P, KV * D], U32)
        v_scales = tile("v_scales", [P, KV * D], U8)
        w_bf = tile("w_bf", [P, TILES, QT, PACK], BF16)
        w_codes = tile("w_codes", [P, GROUPS, TILES * QT], U32)
        w_scales = tile("w_scales", [P, GROUPS, TILES * QT], U8)
        relu_sb = [tile("relu_sb%d" % n, [P, QT, PACK], F32) for n in range(2)]
        y_sb = [tile("y_sb%d" % i, [P, TILES, D], F32) for i in range(GROUPS)]
        table_in = tile("table_in", [P, 1], F32)
        table_out = tile("table_out", [P, 1], F32)
        score_banks = [
            [ps.tile([P, PACK, QT], F32, name="s%d%d" % (g, n)) for n in range(count)]
            for g, count in enumerate(SCORE_BANKS)
        ]
        y_banks = [ps.tile([P, TILES, D], F32, name="y%d" % n) for n in range(Y_BANKS)]
        last = GROUPS - 1

        def load_columns(n):
            c0, count = LOADS[n]
            return slice(c0 * QT, (c0 + count) * QT)

        def load_q(s, n):
            for g0, count in HEAD_RUNS[s]:
                h0 = SETS[s][g0]
                src = qT[h0 : h0 + count, :, load_columns(n)].rearrange("h (p j) q -> (h p) j q", j=PACK)
                nc.sync.dma_start(out=q_raw[s][n][g0 * ROWS : (g0 + count) * ROWS], in_=src)

        def load_mask(n):
            src = mask[:, load_columns(n)].rearrange("(p r) q -> p r q", r=PACK)
            nc.sync.dma_start(out=mask_raw[n][:], in_=src)

        def block(tiles, c):
            n = min(c, len(LOADS) - 1)
            lo = (c - LOADS[n][0]) * QT
            return tiles[n][:, :, lo : lo + QT]

        k_rows = kT.rearrange("k (p j) n -> (k p) j n", j=PACK)
        nc.sync.dma_start(out=k_raw[:ROWS], in_=k_rows[:ROWS])
        nc.scalar.dma_start(out=k_raw[3 * ROWS :], in_=k_rows[ROWS:])
        nc.sync.dma_start(out=k_raw[ROWS : 3 * ROWS], in_=k_rows)
        nc.scalar.dma_start(out=t_sb[:], in_=t.rearrange("(p r) o -> p (r o)", r=PACK))
        for n in range(len(LOADS)):
            load_q(0, n)
            load_mask(n)
            load_q(1, n)
            if n == 1:
                nc.sync.dma_start(out=v_raw[:], in_=v.rearrange("k (p r) e -> p k r e", r=PACK))

        def quantize(codes, scales, src):
            nc.vector.quantize_mx(out=codes.bitcast(FP8X4), scales=scales, in_=src)

        def interleave(dst, src):
            nc.scalar.activation(out=dst, in_=src.rearrange("p j c -> p c j"), func=ACT.Copy)

        def interleave_q(i):
            interleave(q_bf[:, i], block(q_raw[i % 2], i // 2))

        def quantize_q(i):
            quantize(q_codes[:, i], q_scales[:, i], q_bf[:, i].rearrange("p q j -> p (q j)"))

        def quantize_k(r0):
            cols = slice(r0 * P, (r0 + 2) * P)
            quantize(k_codes[:, cols], k_scales[:, cols], k_bf[:, r0 : r0 + 2].rearrange("p r s j -> p (r s j)"))

        def scale_mask(c):
            for r in range(PACK):
                nc.scalar.activation(
                    out=mask_t_rows[c][:, r], in_=block(mask_raw, c)[:, r], func=ACT.Copy, scale=t_sb[:, r : r + 1]
                )

        def interleave_mask(c):
            interleave(mask_t[c][:], mask_t_rows[c][:])

        def interleave_v(k):
            interleave(v_bf[:, k], v_raw[:, k])

        def score_bank(i, g):
            return score_banks[g][i % SCORE_BANKS[g]]

        def scores(i, tiles):
            for r in range(PACK):
                keys = slice(r * P, (r + 1) * P)
                for g in tiles:
                    rows = slice(g * ROWS, (g + 1) * ROWS)
                    nc.tensor.matmul_mx(
                        out=score_bank(i, g)[:, r],
                        lhsT=k_codes[rows, keys].bitcast(FP8X4),
                        lhsT_scale=k_scales[rows, keys],
                        rhs=q_codes[rows, i].bitcast(FP8X4),
                        rhs_scale=q_scales[rows, i],
                        start=True,
                        stop=True,
                    )

        def weights(i, g):
            nc.vector.scalar_tensor_tensor(
                out=w_bf[:, g],
                in0=score_bank(i, g)[:].rearrange("p r q -> p q r"),
                scalar=0.0,
                in1=mask_t[i // 2][:],
                op0=ALU.max,
                op1=ALU.mult,
            )

        def shared_weights(i):
            relu = relu_sb[i % 2]
            src = score_bank(i, SHARED_TILE)[:].rearrange("p r q -> p q r")
            nc.scalar.activation(out=relu[:], in_=src, func=ACT.Relu)
            nc.gpsimd.tensor_tensor(out=w_bf[:, SHARED_TILE], in0=relu[:], in1=mask_t[i // 2][:], op=ALU.mult)

        def quantize_w(i, g0, count):
            cols = slice(g0 * QT, (g0 + count) * QT)
            src = w_bf[:, g0 : g0 + count].rearrange("p g q r -> p (g q r)")
            quantize(w_codes[:, i, cols], w_scales[:, i, cols], src)

        def y_bank(i, g):
            return y_banks[(i + (g // 2 if i == last else 0)) % Y_BANKS]

        def values(i, tiles):
            for g in tiles:
                cols = slice(g * QT, (g + 1) * QT)
                feats = slice(g // 2 * D, (g // 2 + 1) * D)
                nc.tensor.matmul_mx(
                    out=y_bank(i, g)[:, g],
                    lhsT=w_codes[:, i, cols].bitcast(FP8X4),
                    lhsT_scale=w_scales[:, i, cols],
                    rhs=v_codes[:, feats].bitcast(FP8X4),
                    rhs_scale=v_scales[:, feats],
                    start=True,
                    stop=True,
                )

        def store(i, g0, count):
            h0 = SETS[i % 2][g0]
            rows = slice(i // 2 * QT, (i // 2 + 1) * QT)
            dst = out[h0 : h0 + count, rows, :].rearrange("h q e -> q h e")
            nc.sync.dma_start(out=dst, in_=y_sb[i][:, g0 : g0 + count])

        def finish(i):
            nc.scalar.activation(out=y_sb[i][:], in_=y_bank(i, 0)[:], func=ACT.Copy, scale=OUT_SCALE)
            for g0, count in HEAD_RUNS[i % 2]:
                store(i, g0, count)

        nc.vector.memset(table_in[:], 0.0)
        nc.scalar.activation(out=table_out[:], in_=table_in[:], func=ACT.Relu)

        k_in = k_raw[:].rearrange("p j (s r) -> p s j r", r=PACK)
        k_out = k_bf[:].rearrange("p r s j -> p s j r")
        nc.vector.tensor_copy(out=k_out[:, :, :, 0:2], in_=k_in[:, :, :, 0:2])
        nc.scalar.activation(out=k_out[:, :, :, 2:4], in_=k_in[:, :, :, 2:4], func=ACT.Copy)
        nc.vector.tensor_copy(out=q_bf[:, 0], in_=q_raw[0][0][:].rearrange("p j q -> p q j"))
        quantize_k(0)
        quantize_q(0)
        quantize_k(2)
        nc.vector.tensor_tensor(
            out=mask_t[0][:],
            in0=mask_raw[0][:].rearrange("p r q -> p q r"),
            in1=t_sb[:].unsqueeze(1).to_broadcast([P, QT, PACK]),
            op=ALU.mult,
        )
        interleave_q(1)

        values_after_scores = {3: (0, 1), 5: (2, 3), 6: (4, 5), 7: (6,)}
        finish_pair = {step + 1: groups for step, groups in values_after_scores.items() if len(groups) == 2}
        scale_mask_in = {0: 1, 2: 2, 3: 3}
        interleave_mask_in = {1: 1, 3: 2, 5: 3}
        interleave_v_in = {1: 0, 2: 1}
        quantize_v_in = 2
        for i in range(GROUPS):
            scores(i, (SHARED_TILE, 0))
            scores(i, (1, 2))
            if i in finish_pair:
                finish(finish_pair[i][0])
            shared_weights(i)
            if i in interleave_mask_in:
                interleave_mask(interleave_mask_in[i])
            if i + 2 < GROUPS:
                interleave_q(i + 2)
            if i in interleave_v_in:
                interleave_v(interleave_v_in[i])
            if i in scale_mask_in:
                scale_mask(scale_mask_in[i])
            if i in finish_pair:
                finish(finish_pair[i][1])
            for done in values_after_scores.get(i, ()):
                values(done, range(TILES))
            for g in VECTOR_TILES:
                weights(i, g)
                if i == 0 and g == 0:
                    quantize_q(1)
            if i + 2 < GROUPS:
                quantize_q(i + 2)
            if i == quantize_v_in:
                quantize(v_codes[:], v_scales[:], v_bf[:].rearrange("p k e r -> p (k e r)"))
            quantize_w(i, 0, 2)
            if i < last:
                quantize_w(i, 2, 2)

        finish(last - 1)
        values(last, (0, 1))
        nc.scalar.activation(out=y_sb[last][:, 0:2], in_=y_bank(last, 0)[:, 0:2], func=ACT.Copy, scale=OUT_SCALE)
        store(last, 0, 2)
        for g in (3, 2):
            quantize_w(last, g, 1)
        values(last, (3, 2))
        nc.vector.tensor_scalar_mul(y_sb[last][:, 2:4], y_bank(last, 2)[:, 2:4], OUT_SCALE)
        store(last, 2, 2)
